import numpy as np
import ml_dtypes


def mxq(x, axis, fmt="e4m3"):
    dtype, down = {"e4m3": (ml_dtypes.float8_e4m3fn, 7), "e5m2": (ml_dtypes.float8_e5m2, 14)}[fmt]
    v = np.moveaxis(np.asarray(x, np.float32).astype(ml_dtypes.bfloat16).astype(np.float64), axis, -1)
    blocks = v.reshape(v.shape[:-1] + (-1, 32))
    amax = np.abs(blocks).max(-1, keepdims=True)
    byte = np.maximum(np.where(amax > 0, np.frexp(amax)[1] - 1 + 127, 0) - down, 1)
    scale = np.exp2(byte - 127.0)
    codes = (blocks / scale).astype(np.float32).astype(dtype).astype(np.float64)
    return np.moveaxis((codes * scale).reshape(v.shape), -1, axis)


WIDE = False


def mx_kscale(k):
    if not WIDE:
        return np.ones(k)
    levels = np.array([10, -10, 5, -5, 0])
    if k % 512:
        return np.exp2(np.random.permutation(np.resize(levels, k // 32))).repeat(32)
    a = np.empty((k // 512, 16))
    for p in range(k // 512):
        a[p, :8] = np.random.permutation(np.resize(levels, 8))
        for g in range(8):
            far = levels[np.abs(levels - a[p, g]) >= 10]
            a[p, g + 8] = far[np.random.randint(len(far))]
    return np.exp2(a.ravel()).repeat(32)


def f64(x):
    return np.asarray(x).astype(np.float64)


def striped8(idx):
    return np.asarray(idx).reshape(8, -1, 16).transpose(0, 2, 1).reshape(128, -1).astype(np.uint16)


def unstriped8(offs):
    return offs.reshape(8, 16, -1).transpose(0, 2, 1).reshape(8, -1).astype(np.int64)


def pick8(x, idx, run):
    r = np.arange(len(x))
    return x[r[:, None], idx[r % (8 * run) // run]]


E2M1 = np.array([0.0, 0.5, 1.0, 1.5, 2.0, 3.0, 4.0, 6.0, -0.0, -0.5, -1.0, -1.5, -2.0, -3.0, -4.0, -6.0])


def pack_weight(w, fmt):
    k, n = w.shape
    w = f64(np.asarray(w, np.float32).astype(ml_dtypes.bfloat16)).reshape(k // 32, 32, n)
    amax = np.abs(w).max(1)
    if fmt == "e4m3":
        byte = np.frexp(amax)[1] - 1 + 127 - 7
    else:
        mant, ex = np.frexp(amax / 6.0)
        byte = np.where(mant > 0.5, ex, ex - 1) + 127
    byte = np.clip(np.where(amax > 0, byte, 1), 1, 254)
    scaled = (w * np.exp2(127.0 - byte)[:, None, :]).reshape(k, n).astype(np.float32)
    by_word = np.ascontiguousarray(scaled.reshape(k // 512, 128, 4, n).transpose(0, 1, 3, 2))
    if fmt == "e4m3":
        words = by_word.astype(ml_dtypes.float8_e4m3fn).view(np.uint8)
    else:
        c = by_word.astype(ml_dtypes.float4_e2m1fn).view(np.uint8) & 0xF
        words = (c[..., 0::2] | (c[..., 1::2] << 4)).reshape(k // 512, 128, 2 * n)
    return np.ascontiguousarray(words), np.ascontiguousarray(byte.astype(np.uint8).reshape(k // 512, 16, n))


def unpack_weight(words, scales, fmt):
    g, _, n = scales.shape
    words = np.ascontiguousarray(words).reshape(g, 128, n, -1)
    if fmt == "e4m3":
        vals = words.view(ml_dtypes.float8_e4m3fn).astype(np.float64)
    else:
        nib = np.empty((g, 128, n, 4), np.uint8)
        nib[..., 0::2] = words & 0xF
        nib[..., 1::2] = words >> 4
        vals = E2M1[nib]
    vals = vals * np.repeat(np.exp2(scales.astype(np.float64) - 127.0), 8, axis=1)[..., None]
    return vals.transpose(0, 1, 3, 2).reshape(g * 512, n)


D, T, U, X, I, Q = 512, 1024, 1024, 1024, 512, 128


def setup_inputs():
    n = np.random.standard_normal
    idx = np.stack([np.random.permutation(T)[:I] for _ in range(8)])
    idx2 = np.stack([np.random.permutation(U)[:I] for _ in range(8)])
    idx3 = np.stack([np.random.permutation(X)[:I] for _ in range(8)])
    idx4 = np.stack([np.random.permutation(U)[:I] for _ in range(8)])
    idx5 = np.stack([np.random.permutation(T)[:I] for _ in range(8)])
    idx6 = np.stack([np.random.permutation(T)[:I] for _ in range(8)])
    idx7 = np.stack([np.random.permutation(X)[:I] for _ in range(8)])
    fd = mx_kscale(D)
    cachep = pack_weight(n((D, T)) / fd[:, None], "e2m1")
    draftp = pack_weight(n((D, U)) / fd[:, None], "e4m3")
    archp = pack_weight(n((D, X)) / fd[:, None], "e2m1")
    return {
        "query": (n((D, Q)) * 1.0 / np.sqrt(D) * fd[:, None]).astype(np.float32),
        "cache_words": cachep[0],
        "cache_scales": cachep[1],
        "draft_words": draftp[0],
        "draft_scales": draftp[1],
        "arch_words": archp[0],
        "arch_scales": archp[1],
        "offs": striped8(idx),
        "offs2": striped8(idx2),
        "offs3": striped8(idx3),
        "offs4": striped8(idx4),
        "offs5": striped8(idx5),
        "offs6": striped8(idx6),
        "offs7": striped8(idx7),
    }


def reference(query, cache_words, cache_scales, draft_words, draft_scales, arch_words, arch_scales, offs, offs2, offs3, offs4, offs5, offs6, offs7):
    idx = unstriped8(offs)
    idx2 = unstriped8(offs2)
    idx3 = unstriped8(offs3)
    idx4 = unstriped8(offs4)
    idx5 = unstriped8(offs5)
    idx6 = unstriped8(offs6)
    idx7 = unstriped8(offs7)
    cacheu = unpack_weight(cache_words, cache_scales, "e2m1")
    draftu = unpack_weight(draft_words, draft_scales, "e4m3")
    archu = unpack_weight(arch_words, arch_scales, "e2m1")
    queryq = mxq(f64(query), 0, "e4m3")
    a = queryq.T @ cacheu
    b = queryq.T @ draftu
    c0 = queryq.T @ archu
    f1 = np.zeros((Q, U))
    f1[np.arange(Q)[:, None], idx2[np.arange(Q) % 128 // 16]] = pick8(a, idx, 16)
    f2 = np.zeros((Q, X))
    f2[np.arange(Q)[:, None], idx3[np.arange(Q) % 128 // 16]] = pick8(a, idx, 16)
    bb = b + f1
    cc = c0 - f2
    f3 = np.zeros((Q, T))
    f3[np.arange(Q)[:, None], idx5[np.arange(Q) % 128 // 16]] = pick8(bb, idx4, 16)
    aa = a - f3
    y = np.maximum(pick8(aa, idx6, 16), pick8(cc, idx7, 16))
    return y

@@ -1,0 +1,146 @@
+from contextlib import ExitStack
+
+import concourse.mybir as mybir
+
+D, T, I, Q = 512, 1024, 512, 128
+FLOPS = 2 * Q * D * 3 * T
+
+F32 = mybir.dt.float32
+BF16 = mybir.dt.bfloat16
+I32 = mybir.dt.int32
+U32 = mybir.dt.uint32
+U16 = mybir.dt.uint16
+U8 = mybir.dt.uint8
+FP8X4 = mybir.dt.float8_e4m3fn_x4
+FP4X4 = mybir.dt.float4_e2m1fn_x4
+ALU = mybir.AluOpType
+COPY = mybir.ActivationFunctionType.Copy
+
+P = 128
+PACK = 4
+BANK = 512
+A_COLS = 256
+HALF = I // 2
+LANES = 16
+
+
+def tile_attend_fanout_three_kernel(tc, query, cache_words, cache_scales, draft_words, draft_scales,
+                                     arch_words, arch_scales, offs, offs2, offs3, offs4, offs5, offs6, offs7, out):
+    nc = tc.nc
+    with ExitStack() as ctx:
+        keep = ctx.enter_context(tc.tile_pool(name="keep", bufs=1))
+        psum = ctx.enter_context(tc.psum_pool(name="psum", bufs=1))
+
+        def load_list(name, dram):
+            tile = keep.tile([P, I // LANES], U16, name=name)
+            nc.sync.dma_start(tile[:], dram)
+            return tile
+
+        def zeroed_plane(name):
+            plane = keep.tile([P, T], U8, name=name, align_bytes=64)
+            nc.vector.memset(plane[:].bitcast(U32), 0)
+            return plane
+
+        def load_scales(queue, plane, dram):
+            for quad in range(4):
+                queue.dma_start(plane[32 * quad:32 * quad + 4, :].bitcast(I32),
+                                dram[0, 4 * quad:4 * quad + 4, :].bitcast(I32))
+
+        def load_words(name, rows):
+            tile = keep.tile([P, rows.shape[1]], U8, name=name, align_bytes=64)
+            nc.sync.dma_start(tile[:].bitcast(I32), rows.bitcast(I32))
+            return tile
+
+        def zeroed_window(name):
+            window = keep.tile([P, T], F32, name=name)
+            nc.vector.memset(window[:], 0.0)
+            return window
+
+        cache_plane = zeroed_plane("cache_plane")
+        q_raw = keep.tile([P, PACK, Q], F32)
+        nc.sync.dma_start(q_raw[:], query.rearrange("(p j) q -> p j q", j=PACK))
+        load_scales(nc.scalar, cache_plane, cache_scales)
+        cache_codes = load_words("cache_codes", cache_words[0])
+        idx = load_list("idx", offs)
+        idx2 = load_list("idx2", offs2)
+
+        draft_plane = zeroed_plane("draft_plane")
+        arch_plane = zeroed_plane("arch_plane")
+        f1 = zeroed_window("f1")
+        f2 = zeroed_window("f2")
+        f3 = zeroed_window("f3")
+
+        load_scales(nc.sync, draft_plane, draft_scales)
+        draft_codes = load_words("draft_codes", draft_words[0].rearrange("p n t -> p (n t)"))
+        idx3 = load_list("idx3", offs3)
+        idx4 = load_list("idx4", offs4)
+        load_scales(nc.sync, arch_plane, arch_scales)
+        arch_codes = load_words("arch_codes", arch_words[0])
+        idx5 = load_list("idx5", offs5)
+        idx7 = load_list("idx7", offs7)
+        idx6 = load_list("idx6", offs6)
+
+        q_grouped = keep.tile([P, Q, PACK], BF16, align_bytes=64)
+        nc.vector.tensor_copy(q_grouped[:].rearrange("p (c i) t -> p c t i", i=4),
+                              q_raw[:].rearrange("p t (c i) -> p c t i", i=4))
+        q_codes = keep.tile([P, Q], U32, align_bytes=64)
+        q_plane = keep.tile([P, Q], U8, align_bytes=64)
+        nc.vector.quantize_mx(out=q_codes[:].bitcast(FP8X4), scales=q_plane[:],
+                              in_=q_grouped[:].rearrange("p q t -> p (q t)"))
+
+        def score(name, codes, plane, word_bytes, fmt, width):
+            banks = []
+            for c0 in range(0, T, width):
+                bank = psum.tile([P, width], F32, name=name + str(c0 // width))
+                nc.tensor.matmul_mx(out=bank[:], lhsT=q_codes[:].bitcast(FP8X4), lhsT_scale=q_plane[:],
+                                    rhs=codes[:, word_bytes * c0:word_bytes * (c0 + width)].bitcast(fmt),
+                                    rhs_scale=plane[:, c0:c0 + width], start=True, stop=True)
+                banks.append(bank)
+            return banks
+
+        a_banks = score("a_bank", cache_codes, cache_plane, 2, FP4X4, A_COLS)
+        b_banks = score("b_bank", draft_codes, draft_plane, 4, FP8X4, BANK)
+        c_banks = score("c_bank", arch_codes, arch_plane, 2, FP4X4, BANK)
+
+        a = keep.tile([P, T], F32)
+        for n, bank in enumerate(a_banks):
+            cols = slice(n * A_COLS, (n + 1) * A_COLS)
+            if n % 2 == 0:
+                nc.vector.tensor_copy(a[:, cols], bank[:])
+            else:
+                nc.scalar.activation(a[:, cols], bank[:], COPY)
+
+        halves = [(slice(h * HALF, (h + 1) * HALF), slice(h * HALF // LANES, (h + 1) * HALF // LANES)) for h in range(2)]
+
+        a_picked = keep.tile([P, I], F32)
+        for slots, entries in halves:
+            nc.vector.tensor_copy(a_picked[:, slots], a[:].indirect(idx[:, entries]))
+        for slots, entries in halves:
+            nc.scalar.activation(f1[:].indirect(idx2[:, entries]), a_picked[:, slots], COPY)
+        nc.scalar.activation(f2[:].indirect(idx3[:]), a_picked[:], COPY)
+
+        bb = keep.tile([P, T], F32, tag="sums")
+        for n, bank in enumerate(b_banks):
+            cols = slice(n * BANK, (n + 1) * BANK)
+            nc.vector.tensor_tensor(bb[:, cols], bank[:], f1[:, cols], ALU.add)
+        bb_picked = keep.tile([P, I], F32)
+        nc.vector.tensor_copy(bb_picked[:], bb[:].indirect(idx4[:]))
+        nc.scalar.activation(f3[:].indirect(idx5[:]), bb_picked[:], COPY)
+
+        cc = keep.tile([P, T], F32, tag="sums")
+        for n, bank in enumerate(c_banks):
+            cols = slice(n * BANK, (n + 1) * BANK)
+            nc.vector.tensor_tensor(cc[:, cols], bank[:], f2[:, cols], ALU.subtract)
+        cc_picked = keep.tile([P, I], F32)
+        nc.vector.tensor_copy(cc_picked[:], cc[:].indirect(idx7[:]))
+
+        aa = keep.tile([P, T], F32, tag="sums")
+        nc.vector.tensor_tensor(aa[:], a[:], f3[:], ALU.subtract)
+        aa_picked = keep.tile([P, I], F32)
+        (slots0, entries0), (slots1, entries1) = halves
+        nc.vector.tensor_copy(aa_picked[:, slots0], aa[:].indirect(idx6[:, entries0]))
+        nc.scalar.activation(aa_picked[:, slots1], aa[:].indirect(idx6[:, entries1]), COPY)
+        result = keep.tile([P, I], F32)
+        for slots, entries in halves:
+            nc.vector.tensor_tensor(result[:, slots], aa_picked[:, slots], cc_picked[:, slots], ALU.max)
+            nc.sync.dma_start(out[:, slots], result[:, slots])

@@ -19,7 +19,7 @@ COPY = mybir.ActivationFunctionType.Copy
 P = 128
 PACK = 4
 BANK = 512
-A_COLS = 256
+A_WIDTHS = (512, 256, 256)
 HALF = I // 2
 LANES = 16
 
@@ -47,12 +47,12 @@ def tile_attend_fanout_three_kernel(tc, query, cache_words, cache_scales, draft_
                                 dram[0, 4 * quad:4 * quad + 4, :].bitcast(I32))
 
         def load_words(name, rows):
-            tile = keep.tile([P, rows.shape[1]], U8, name=name, align_bytes=64)
+            tile = keep.tile([P, rows.shape[1]], U8, name=name, tag=name, align_bytes=64)
             nc.sync.dma_start(tile[:].bitcast(I32), rows.bitcast(I32))
             return tile
 
-        def zeroed_window(name):
-            window = keep.tile([P, T], F32, name=name)
+        def zeroed_window(name, tag):
+            window = keep.tile([P, T], F32, name=name, tag=tag, align_bytes=64)
             nc.vector.memset(window[:], 0.0)
             return window
 
@@ -66,12 +66,12 @@ def tile_attend_fanout_three_kernel(tc, query, cache_words, cache_scales, draft_
 
         draft_plane = zeroed_plane("draft_plane")
         arch_plane = zeroed_plane("arch_plane")
-        f1 = zeroed_window("f1")
-        f2 = zeroed_window("f2")
-        f3 = zeroed_window("f3")
+        f1 = zeroed_window("f1", "f1")
 
         load_scales(nc.sync, draft_plane, draft_scales)
-        draft_codes = load_words("draft_codes", draft_words[0].rearrange("p n t -> p (n t)"))
+        draft_rows = draft_words[0].rearrange("p n t -> p (n t)")
+        draft_parts = [(c0, width, load_words("draft_codes" + str(c0), draft_rows[:, 4 * c0:4 * (c0 + width)]))
+                       for c0, width in ((0, 512), (512, 512))]
         idx3 = load_list("idx3", offs3)
         idx4 = load_list("idx4", offs4)
         load_scales(nc.sync, arch_plane, arch_scales)
@@ -88,24 +88,26 @@ def tile_attend_fanout_three_kernel(tc, query, cache_words, cache_scales, draft_
         nc.vector.quantize_mx(out=q_codes[:].bitcast(FP8X4), scales=q_plane[:],
                               in_=q_grouped[:].rearrange("p q t -> p (q t)"))
 
-        def score(name, codes, plane, word_bytes, fmt, width):
-            banks = []
-            for c0 in range(0, T, width):
-                bank = psum.tile([P, width], F32, name=name + str(c0 // width))
-                nc.tensor.matmul_mx(out=bank[:], lhsT=q_codes[:].bitcast(FP8X4), lhsT_scale=q_plane[:],
-                                    rhs=codes[:, word_bytes * c0:word_bytes * (c0 + width)].bitcast(fmt),
-                                    rhs_scale=plane[:, c0:c0 + width], start=True, stop=True)
-                banks.append(bank)
-            return banks
+        def score(bank, codes, fmt, plane):
+            nc.tensor.matmul_mx(out=bank, lhsT=q_codes[:].bitcast(FP8X4), lhsT_scale=q_plane[:],
+                                rhs=codes.bitcast(fmt), rhs_scale=plane, start=True, stop=True)
 
-        a_banks = score("a_bank", cache_codes, cache_plane, 2, FP4X4, A_COLS)
-        b_banks = score("b_bank", draft_codes, draft_plane, 4, FP8X4, BANK)
-        c_banks = score("c_bank", arch_codes, arch_plane, 2, FP4X4, BANK)
+        a_banks = [(sum(A_WIDTHS[:n]), width, psum.tile([P, width], F32, name="a_bank" + str(n)))
+                   for n, width in enumerate(A_WIDTHS)]
+        b_banks = [psum.tile([P, BANK], F32, name="b_bank" + str(n)) for n in range(T // BANK)]
+        c_banks = [psum.tile([P, BANK], F32, name="c_bank" + str(n)) for n in range(T // BANK)]
+        for c0, width, bank in a_banks:
+            score(bank[:], cache_codes[:, 2 * c0:2 * (c0 + width)], FP4X4, cache_plane[:, c0:c0 + width])
+        for c0, width, codes in draft_parts:
+            score(b_banks[c0 // BANK][:, c0 % BANK:c0 % BANK + width], codes[:], FP8X4, draft_plane[:, c0:c0 + width])
+        for n, bank in enumerate(c_banks):
+            c0 = n * BANK
+            score(bank[:], arch_codes[:, 2 * c0:2 * (c0 + BANK)], FP4X4, arch_plane[:, c0:c0 + BANK])
 
-        a = keep.tile([P, T], F32)
-        for n, bank in enumerate(a_banks):
-            cols = slice(n * A_COLS, (n + 1) * A_COLS)
-            if n % 2 == 0:
+        a = keep.tile([P, T], F32, tag="a", align_bytes=64)
+        for c0, width, bank in a_banks:
+            cols = slice(c0, c0 + width)
+            if c0 == 0:
                 nc.vector.tensor_copy(a[:, cols], bank[:])
             else:
                 nc.scalar.activation(a[:, cols], bank[:], COPY)
@@ -117,6 +119,8 @@ def tile_attend_fanout_three_kernel(tc, query, cache_words, cache_scales, draft_
             nc.vector.tensor_copy(a_picked[:, slots], a[:].indirect(idx[:, entries]))
         for slots, entries in halves:
             nc.scalar.activation(f1[:].indirect(idx2[:, entries]), a_picked[:, slots], COPY)
+        f2 = zeroed_window("f2", "draft_codes0")
+        f3 = zeroed_window("f3", "a")
         nc.scalar.activation(f2[:].indirect(idx3[:]), a_picked[:], COPY)
 
         bb = keep.tile([P, T], F32, tag="sums")
@@ -135,7 +139,8 @@ def tile_attend_fanout_three_kernel(tc, query, cache_words, cache_scales, draft_
         nc.vector.tensor_copy(cc_picked[:], cc[:].indirect(idx7[:]))
 
         aa = keep.tile([P, T], F32, tag="sums")
-        nc.vector.tensor_tensor(aa[:], a[:], f3[:], ALU.subtract)
+        for c0, width, bank in a_banks:
+            nc.vector.tensor_tensor(aa[:, c0:c0 + width], bank[:], f3[:, c0:c0 + width], ALU.subtract)
         aa_picked = keep.tile([P, I], F32)
         (slots0, entries0), (slots1, entries1) = halves
         nc.vector.tensor_copy(aa_picked[:, slots0], aa[:].indirect(idx6[:, entries0]))

from contextlib import ExitStack

import concourse.mybir as mybir

D, T, I, Q = 512, 1024, 512, 128
FLOPS = 2 * Q * D * 3 * T

F32 = mybir.dt.float32
BF16 = mybir.dt.bfloat16
I32 = mybir.dt.int32
U32 = mybir.dt.uint32
U16 = mybir.dt.uint16
U8 = mybir.dt.uint8
FP8X4 = mybir.dt.float8_e4m3fn_x4
FP4X4 = mybir.dt.float4_e2m1fn_x4
ALU = mybir.AluOpType
COPY = mybir.ActivationFunctionType.Copy

P = 128
PACK = 4
BANK = 512
A_WIDTHS = (512, 256, 256)
HALF = I // 2
LANES = 16


def tile_attend_fanout_three_kernel(tc, query, cache_words, cache_scales, draft_words, draft_scales,
                                     arch_words, arch_scales, offs, offs2, offs3, offs4, offs5, offs6, offs7, out):
    nc = tc.nc
    with ExitStack() as ctx:
        keep = ctx.enter_context(tc.tile_pool(name="keep", bufs=1))
        psum = ctx.enter_context(tc.psum_pool(name="psum", bufs=1))

        def load_list(name, dram):
            tile = keep.tile([P, I // LANES], U16, name=name)
            nc.sync.dma_start(tile[:], dram)
            return tile

        def zeroed_plane(name):
            plane = keep.tile([P, T], U8, name=name, align_bytes=64)
            nc.vector.memset(plane[:].bitcast(U32), 0)
            return plane

        def load_scales(queue, plane, dram):
            for quad in range(4):
                queue.dma_start(plane[32 * quad:32 * quad + 4, :].bitcast(I32),
                                dram[0, 4 * quad:4 * quad + 4, :].bitcast(I32))

        def load_words(name, rows):
            tile = keep.tile([P, rows.shape[1]], U8, name=name, tag=name, align_bytes=64)
            nc.sync.dma_start(tile[:].bitcast(I32), rows.bitcast(I32))
            return tile

        def zeroed_window(name, tag):
            window = keep.tile([P, T], F32, name=name, tag=tag, align_bytes=64)
            nc.vector.memset(window[:], 0.0)
            return window

        cache_plane = zeroed_plane("cache_plane")
        q_raw = keep.tile([P, PACK, Q], F32)
        nc.sync.dma_start(q_raw[:], query.rearrange("(p j) q -> p j q", j=PACK))
        load_scales(nc.scalar, cache_plane, cache_scales)
        cache_codes = load_words("cache_codes", cache_words[0])
        idx = load_list("idx", offs)
        idx2 = load_list("idx2", offs2)

        draft_plane = zeroed_plane("draft_plane")
        arch_plane = zeroed_plane("arch_plane")
        f1 = zeroed_window("f1", "f1")

        load_scales(nc.sync, draft_plane, draft_scales)
        draft_rows = draft_words[0].rearrange("p n t -> p (n t)")
        draft_parts = [(c0, width, load_words("draft_codes" + str(c0), draft_rows[:, 4 * c0:4 * (c0 + width)]))
                       for c0, width in ((0, 512), (512, 512))]
        idx3 = load_list("idx3", offs3)
        idx4 = load_list("idx4", offs4)
        load_scales(nc.sync, arch_plane, arch_scales)
        arch_codes = load_words("arch_codes", arch_words[0])
        idx5 = load_list("idx5", offs5)
        idx7 = load_list("idx7", offs7)
        idx6 = load_list("idx6", offs6)

        q_grouped = keep.tile([P, Q, PACK], BF16, align_bytes=64)
        nc.vector.tensor_copy(q_grouped[:].rearrange("p (c i) t -> p c t i", i=4),
                              q_raw[:].rearrange("p t (c i) -> p c t i", i=4))
        q_codes = keep.tile([P, Q], U32, align_bytes=64)
        q_plane = keep.tile([P, Q], U8, align_bytes=64)
        nc.vector.quantize_mx(out=q_codes[:].bitcast(FP8X4), scales=q_plane[:],
                              in_=q_grouped[:].rearrange("p q t -> p (q t)"))

        def score(bank, codes, fmt, plane):
            nc.tensor.matmul_mx(out=bank, lhsT=q_codes[:].bitcast(FP8X4), lhsT_scale=q_plane[:],
                                rhs=codes.bitcast(fmt), rhs_scale=plane, start=True, stop=True)

        a_banks = [(sum(A_WIDTHS[:n]), width, psum.tile([P, width], F32, name="a_bank" + str(n)))
                   for n, width in enumerate(A_WIDTHS)]
        b_banks = [psum.tile([P, BANK], F32, name="b_bank" + str(n)) for n in range(T // BANK)]
        c_banks = [psum.tile([P, BANK], F32, name="c_bank" + str(n)) for n in range(T // BANK)]
        for c0, width, bank in a_banks:
            score(bank[:], cache_codes[:, 2 * c0:2 * (c0 + width)], FP4X4, cache_plane[:, c0:c0 + width])
        for c0, width, codes in draft_parts:
            score(b_banks[c0 // BANK][:, c0 % BANK:c0 % BANK + width], codes[:], FP8X4, draft_plane[:, c0:c0 + width])
        for n, bank in enumerate(c_banks):
            c0 = n * BANK
            score(bank[:], arch_codes[:, 2 * c0:2 * (c0 + BANK)], FP4X4, arch_plane[:, c0:c0 + BANK])

        a = keep.tile([P, T], F32, tag="a", align_bytes=64)
        for c0, width, bank in a_banks:
            cols = slice(c0, c0 + width)
            if c0 == 0:
                nc.vector.tensor_copy(a[:, cols], bank[:])
            else:
                nc.scalar.activation(a[:, cols], bank[:], COPY)

        halves = [(slice(h * HALF, (h + 1) * HALF), slice(h * HALF // LANES, (h + 1) * HALF // LANES)) for h in range(2)]

        a_picked = keep.tile([P, I], F32)
        for slots, entries in halves:
            nc.vector.tensor_copy(a_picked[:, slots], a[:].indirect(idx[:, entries]))
        for slots, entries in halves:
            nc.scalar.activation(f1[:].indirect(idx2[:, entries]), a_picked[:, slots], COPY)
        f2 = zeroed_window("f2", "draft_codes0")
        f3 = zeroed_window("f3", "a")
        nc.scalar.activation(f2[:].indirect(idx3[:]), a_picked[:], COPY)

        bb = keep.tile([P, T], F32, tag="sums")
        for n, bank in enumerate(b_banks):
            cols = slice(n * BANK, (n + 1) * BANK)
            nc.vector.tensor_tensor(bb[:, cols], bank[:], f1[:, cols], ALU.add)
        bb_picked = keep.tile([P, I], F32)
        nc.vector.tensor_copy(bb_picked[:], bb[:].indirect(idx4[:]))
        nc.scalar.activation(f3[:].indirect(idx5[:]), bb_picked[:], COPY)

        cc = keep.tile([P, T], F32, tag="sums")
        for n, bank in enumerate(c_banks):
            cols = slice(n * BANK, (n + 1) * BANK)
            nc.vector.tensor_tensor(cc[:, cols], bank[:], f2[:, cols], ALU.subtract)
        cc_picked = keep.tile([P, I], F32)
        nc.vector.tensor_copy(cc_picked[:], cc[:].indirect(idx7[:]))

        aa = keep.tile([P, T], F32, tag="sums")
        for c0, width, bank in a_banks:
            nc.vector.tensor_tensor(aa[:, c0:c0 + width], bank[:], f3[:, c0:c0 + width], ALU.subtract)
        aa_picked = keep.tile([P, I], F32)
        (slots0, entries0), (slots1, entries1) = halves
        nc.vector.tensor_copy(aa_picked[:, slots0], aa[:].indirect(idx6[:, entries0]))
        nc.scalar.activation(aa_picked[:, slots1], aa[:].indirect(idx6[:, entries1]), COPY)
        result = keep.tile([P, I], F32)
        for slots, entries in halves:
            nc.vector.tensor_tensor(result[:, slots], aa_picked[:, slots], cc_picked[:, slots], ALU.max)
            nc.sync.dma_start(out[:, slots], result[:, slots])
